import numpy as np
import ml_dtypes


def mxq(x, axis, fmt="e4m3"):
    dtype, down = {"e4m3": (ml_dtypes.float8_e4m3fn, 7), "e5m2": (ml_dtypes.float8_e5m2, 14)}[fmt]
    v = np.moveaxis(np.asarray(x, np.float32).astype(ml_dtypes.bfloat16).astype(np.float64), axis, -1)
    blocks = v.reshape(v.shape[:-1] + (-1, 32))
    amax = np.abs(blocks).max(-1, keepdims=True)
    byte = np.maximum(np.where(amax > 0, np.frexp(amax)[1] - 1 + 127, 0) - down, 1)
    scale = np.exp2(byte - 127.0)
    codes = (blocks / scale).astype(np.float32).astype(dtype).astype(np.float64)
    return np.moveaxis((codes * scale).reshape(v.shape), -1, axis)


WIDE = False


def mx_kscale(k):
    if not WIDE:
        return np.ones(k)
    levels = np.array([18, -18])
    if k % 512:
        return np.exp2(np.random.permutation(np.resize(levels, k // 32))).repeat(32)
    a = np.empty((k // 512, 16))
    for p in range(k // 512):
        a[p, :8] = np.random.permutation(np.resize(levels, 8))
        for g in range(8):
            far = levels[np.abs(levels - a[p, g]) >= 10]
            a[p, g + 8] = far[np.random.randint(len(far))]
    return np.exp2(a.ravel()).repeat(32)


def f64(x):
    return np.asarray(x).astype(np.float64)


def striped(idx):
    return np.tile(np.asarray(idx).reshape(-1, 16).T, (8, 1)).astype(np.uint16)


def unstriped(offs):
    return offs[:16].T.reshape(-1).astype(np.int64)

def planes(y):
    n, m = y.shape
    v = y.astype(np.float32).astype(ml_dtypes.bfloat16).astype(np.float64).reshape(n // 32, 32, m)
    top = np.abs(v).max(1)
    byte = np.clip(np.where(top > 0, np.frexp(top)[1] - 1 + 127 - 7, 1), 1, 254)
    codes = (v * np.exp2(127.0 - byte)[:, None, :]).reshape(n, m).astype(np.float32).astype(ml_dtypes.float8_e4m3fn).view(np.uint8)
    words = codes.reshape(n // 512, 128, 4, m).transpose(0, 1, 3, 2)
    return np.ascontiguousarray(words), np.ascontiguousarray(byte.astype(np.uint8).reshape(n // 512, 16, m))


B, N, T, D, DV = 1, 1024, 2048, 512, 512


def setup_inputs():
    n = np.random.standard_normal
    idx = np.random.permutation(T)[:B * N]
    v = mx_kscale(DV)[:, None]
    coarse = lambda x: x.astype(np.float32).astype(ml_dtypes.bfloat16).astype(np.float64)
    r = np.random.randint(8, 33, T) / 16.0
    return {
        "dyT": (coarse(n((DV, T))) * v).astype(np.float32),
        "hT": coarse(n((DV, T))).astype(np.float32),
        "ts": np.tile(r, (128, 1)).astype(np.float32),
        "wm": (n((B, DV, D)) / np.sqrt(DV) / v).astype(np.float32),
        "offs": striped(idx),
    }


def reference(dyT, hT, ts, wm, offs):
    idx = unstriped(offs)
    pick = lambda x: x[:, idx].reshape(x.shape[0], B, N).transpose(1, 0, 2)
    h = pick(f64(hT))
    dz = pick(f64(ts))[:, :1, :] * pick(f64(dyT)) * 2.0 * np.maximum(h, 0.0)
    dx = mxq(f64(wm), 1, "e4m3").transpose(0, 2, 1) @ mxq(dz, 1, "e5m2")
    gx = np.zeros((D, T))
    gx[:, idx] = dx.transpose(1, 0, 2).reshape(D, B * N)
    out_0 = gx
    return (out_0,) + planes(out_0)

@@ -1,0 +1,192 @@
+from contextlib import ExitStack
+
+import concourse.mybir as mybir
+from concourse.masks import make_identity
+
+T, N, D, DV = 2048, 1024, 512, 512
+FLOPS = 2 * N * D * DV
+
+F32 = mybir.dt.float32
+BF16 = mybir.dt.bfloat16
+I32 = mybir.dt.int32
+U32 = mybir.dt.uint32
+U16 = mybir.dt.uint16
+U8 = mybir.dt.uint8
+E4M3 = mybir.dt.float8_e4m3fn_x4
+E5M2 = mybir.dt.float8_e5m2_x4
+COPY = mybir.ActivationFunctionType.Copy
+MULT = mybir.AluOpType.mult
+MAX = mybir.AluOpType.max
+
+P = 128
+PACK = 4
+HALF = N // 2
+BANK = 512
+PIECE = 256
+CHUNK = 512
+
+
+def tile_attend_gex_pl_x_kernel(tc, dyT, hT, ts, wm, offs, out_0, out_1, out_2):
+    nc = tc.nc
+    with ExitStack() as ctx:
+        keep = ctx.enter_context(tc.tile_pool(name="keep", bufs=1))
+        ring = ctx.enter_context(tc.tile_pool(name="ring", bufs=2))
+        psum = ctx.enter_context(tc.psum_pool(name="psum", bufs=4))
+        single = ctx.enter_context(tc.psum_pool(name="single", bufs=1))
+
+        def slots(first, count):
+            return offsets[:, first // 16 : (first + count) // 16]
+
+        offsets = keep.tile([P, N // 16], U16, name="offsets")
+        nc.sync.dma_start(offsets[:], offs)
+        ts_cols = keep.tile([P, T // P], F32, name="ts_cols")
+        nc.sync.dma_start(ts_cols[:], ts[0].rearrange("(p c) -> p c", p=P))
+        w_raw = keep.tile([P, PACK, D], F32, name="w_raw")
+        nc.sync.dma_start(w_raw[:], wm[0].rearrange("(p j) d -> p j d", j=PACK))
+        h_planes = hT.rearrange("(p t) c -> t p c", t=PACK)
+        dy_planes = dyT.rearrange("(p t) c -> t p c", t=PACK)
+        h_win = []
+        dy_win = []
+        for t in range(PACK):
+            h_win.append(keep.tile([P, T], F32, name="h_win%d" % t))
+            nc.sync.dma_start(h_win[t][:], h_planes[t])
+            dy_win.append(keep.tile([P, T], F32, name="dy_win%d" % t))
+            nc.sync.dma_start(dy_win[t][:], dy_planes[t])
+
+        identity = keep.tile([P, P], F32, name="identity")
+        make_identity(nc, identity[:])
+        placed = []
+        for t in range(PACK):
+            placed.append(keep.tile([P, T], F32, name="placed%d" % t))
+            nc.vector.memset(placed[t][:], 0.0)
+
+        w_grouped = keep.tile([P, PACK, P, PACK], BF16, name="w_grouped", align_bytes=64)
+        nc.vector.tensor_copy(
+            w_grouped[:], w_raw[:].rearrange("p j (m t) -> p t m j", t=PACK)
+        )
+        w_codes = keep.tile([P, D], U32, name="w_codes", align_bytes=64)
+        w_scales = keep.tile([P, D], U8, name="w_scales", align_bytes=64)
+        nc.vector.quantize_mx(w_codes[:].bitcast(E4M3), w_scales[:], w_grouped[:].rearrange("p t m j -> p (t m j)"))
+
+        ts_win = keep.tile([P, T], F32, name="ts_win", tag="ts_win")
+        ts_lines = ts_win[:].rearrange("q (p b c) -> q b p c", p=P, c=BANK // P)
+        for b in range(T // BANK):
+            spread = psum.tile([P, BANK // P, P], F32, name="spread")
+            for c in range(BANK // P):
+                col = b * (BANK // P) + c
+                nc.tensor.transpose(spread[:, c, :], ts_cols[:, col : col + 1].to_broadcast([P, P]), identity[:])
+            nc.scalar.activation(ts_lines[:, b], spread[:].rearrange("q c p -> q p c"), COPY)
+
+        ts2 = keep.tile([P, N], F32, name="ts2")
+        nc.scalar.activation(ts2[:], ts_win[:].indirect(offsets[:]), COPY, scale=2.0)
+        dz_first = keep.tile([P, PACK, HALF], F32, name="dz_first")
+        dz_second = keep.tile([P, PACK, HALF], BF16, name="dz_second")
+
+        h_picked = ring.tile([P, N], F32, name="h_picked")
+        nc.vector.tensor_copy(h_picked[:], h_win[0][:].indirect(offsets[:]))
+        dy_all = keep.tile([P, N], F32, name="dy_all")
+        nc.vector.tensor_copy(dy_all[:], dy_win[0][:].indirect(offsets[:]))
+        partial = ring.tile([P, N], F32, name="partial")
+        nc.vector.scalar_tensor_tensor(partial[:], h_picked[:], 0.0, dy_all[:], MAX, MULT)
+        nc.vector.tensor_tensor(dz_first[:, 0, :], partial[:, 0:HALF], ts2[:, 0:HALF], MULT)
+        nc.vector.tensor_tensor(dz_second[:, 0, :], partial[:, HALF:N], ts2[:, HALF:N], MULT)
+
+        for t in range(1, PACK):
+            if t == 1:
+                h_picked = keep.tile([P, N], F32, name="h_picked", tag="ts_win")
+            else:
+                h_picked = ring.tile([P, N], F32, name="h_picked")
+            if t < PACK - 1:
+                nc.scalar.activation(h_picked[:], h_win[t][:].indirect(offsets[:]), COPY)
+            else:
+                nc.vector.tensor_copy(h_picked[:, 0:HALF], h_win[t][:].indirect(slots(0, HALF)))
+                nc.scalar.activation(h_picked[:, HALF:N], h_win[t][:].indirect(slots(HALF, HALF)), COPY)
+            dy_picked = ring.tile([P, HALF], F32, name="dy_picked")
+            nc.scalar.activation(dy_picked[:], dy_win[t][:].indirect(slots(HALF, HALF)), COPY)
+            partial = ring.tile([P, N], F32, name="partial")
+            nc.vector.scalar_tensor_tensor(partial[:], h_picked[:], 0.0, ts2[:], MAX, MULT)
+            nc.vector.tensor_tensor(dz_first[:, t, :], dy_win[t][:].indirect(slots(0, HALF)), partial[:, 0:HALF], MULT)
+            if t < PACK - 1:
+                nc.vector.tensor_tensor(dz_second[:, t, :], dy_picked[:], partial[:, HALF:N], MULT)
+
+        def group_dz(planes, half, copy):
+            grouped = keep.tile([P, HALF, PACK], BF16, name="grouped%d" % half, align_bytes=64)
+            copy(
+                grouped[:], planes[:].rearrange("p t s -> p s t")
+            )
+            codes = keep.tile([P, HALF], U32, name="dz_codes%d" % half, align_bytes=64)
+            scales = keep.tile([P, HALF], U8, name="dz_scales%d" % half, align_bytes=64)
+            return grouped, codes, scales
+
+        nc.vector.tensor_tensor(dz_second[:, PACK - 1, :], dy_picked[:], partial[:, HALF:N], MULT)
+        first = group_dz(dz_first, 0, nc.vector.tensor_copy)
+        second = group_dz(dz_second, 1, nc.scalar.copy)
+        nc.vector.quantize_mx(first[1][:].bitcast(E5M2), first[2][:], first[0][:].rearrange("p s t -> p (s t)"))
+        nc.vector.quantize_mx(second[1][:].bitcast(E5M2), second[2][:], second[0][:].rearrange("p s t -> p (s t)"))
+        operands = (first, second)
+
+        def product(t, half, tag):
+            bank = single.tile([P, BANK], F32, name="product", tag=tag)
+            nc.tensor.matmul_mx(
+                bank[:],
+                lhsT=w_codes[:, t * P : (t + 1) * P].bitcast(E4M3),
+                lhsT_scale=w_scales[:, t * P : (t + 1) * P],
+                rhs=operands[half][1][:].bitcast(E5M2),
+                rhs_scale=operands[half][2][:],
+                start=True,
+                stop=True,
+            )
+            return bank
+
+        def scatter_on_scalar(t, half):
+            bank = product(t, half, "scalar_bank")
+            dx = ring.tile([P, HALF], F32, name="dx_scalar")
+            nc.scalar.copy(dx[:], bank[:])
+            for first_slot in range(0, HALF, PIECE):
+                nc.scalar.activation(
+                    placed[t][:].indirect(slots(half * HALF + first_slot, PIECE)),
+                    dx[:, first_slot : first_slot + PIECE],
+                    COPY,
+                )
+
+        def scatter_on_vector(t, half):
+            bank = product(t, half, "vector_bank")
+            dx = ring.tile([P, HALF], F32, name="dx_vector")
+            nc.vector.tensor_copy(dx[:], bank[:])
+            nc.vector.tensor_copy(placed[t][:].indirect(slots(half * HALF, HALF)), dx[:])
+
+        out_planes = out_0.rearrange("(p t) c -> t p c", t=PACK)
+        pairs = [keep.tile([P, 2, CHUNK, 2], BF16, name="pairs%d" % c) for c in range(T // CHUNK)]
+
+        def hand_out(t):
+            nc.sync.dma_start(out_planes[t], placed[t][:])
+            for c in range(T // CHUNK):
+                nc.vector.tensor_copy(pairs[c][:, t // 2, :, t % 2], placed[t][:, c * CHUNK : (c + 1) * CHUNK])
+
+        scatter_on_scalar(0, 0)
+        scatter_on_vector(1, 0)
+        scatter_on_scalar(0, 1)
+        scatter_on_vector(1, 1)
+        scatter_on_scalar(2, 0)
+        hand_out(0)
+        hand_out(1)
+        scatter_on_scalar(3, 0)
+        scatter_on_vector(2, 1)
+        scatter_on_scalar(3, 1)
+        hand_out(2)
+        hand_out(3)
+
+        out_words = out_1[0].rearrange("p t l -> p (t l)").bitcast(I32)
+        y_scales = keep.tile([P, T], U8, name="y_scales", align_bytes=64)
+        for c in range(T // CHUNK):
+            y_grouped = keep.tile([P, CHUNK * PACK], BF16, name="y_grouped%d" % c, align_bytes=64)
+            nc.scalar.copy(
+                y_grouped[:].bitcast(U32).rearrange("p (s u) -> p s u", u=2),
+                pairs[c][:].rearrange("p u s e -> p u (s e)").bitcast(U32).rearrange("p u s -> p s u"),
+            )
+            y_codes = keep.tile([P, CHUNK], U32, name="y_codes%d" % c, align_bytes=64)
+            nc.vector.quantize_mx(y_codes[:].bitcast(E4M3), y_scales[:, c * CHUNK : (c + 1) * CHUNK], y_grouped[:])
+            nc.sync.dma_start(out_words[:, c * CHUNK : (c + 1) * CHUNK], y_codes[:].bitcast(I32))
+        scale_rows = out_2[0].bitcast(I32)
+        for q in range(4):
+            nc.sync.dma_start(scale_rows[4 * q : 4 * q + 4, :], y_scales[32 * q : 32 * q + 4, :].bitcast(I32))

@@ -24,6 +24,9 @@ HALF = N // 2
 BANK = 512
 PIECE = 256
 CHUNK = 512
+H_ON_VECTOR = (N, 256, 256, 384)
+DY_ON_VECTOR = (384, 384, 384, HALF)
+SHARED = 256
 
 
 def tile_attend_gex_pl_x_kernel(tc, dyT, hT, ts, wm, offs, out_0, out_1, out_2):
@@ -45,28 +48,33 @@ def tile_attend_gex_pl_x_kernel(tc, dyT, hT, ts, wm, offs, out_0, out_1, out_2):
         nc.sync.dma_start(w_raw[:], wm[0].rearrange("(p j) d -> p j d", j=PACK))
         h_planes = hT.rearrange("(p t) c -> t p c", t=PACK)
         dy_planes = dyT.rearrange("(p t) c -> t p c", t=PACK)
-        h_win = []
-        dy_win = []
-        for t in range(PACK):
-            h_win.append(keep.tile([P, T], F32, name="h_win%d" % t))
-            nc.sync.dma_start(h_win[t][:], h_planes[t])
-            dy_win.append(keep.tile([P, T], F32, name="dy_win%d" % t))
-            nc.sync.dma_start(dy_win[t][:], dy_planes[t])
+        h_win = [keep.tile([P, T], F32, name="h_win%d" % t) for t in range(PACK)]
+        dy_win = [keep.tile([P, T], F32, name="dy_win%d" % t) for t in range(PACK)]
+        for step in range(PACK + 1):
+            if step < PACK:
+                nc.sync.dma_start(h_win[step][:], h_planes[step])
+            if step > 0:
+                nc.sync.dma_start(dy_win[step - 1][:], dy_planes[step - 1])
 
         identity = keep.tile([P, P], F32, name="identity")
         make_identity(nc, identity[:])
         placed = []
         for t in range(PACK):
             placed.append(keep.tile([P, T], F32, name="placed%d" % t))
-            nc.vector.memset(placed[t][:], 0.0)
+            nc.vector.memset(placed[t][:].bitcast(I32), 0)
 
-        w_grouped = keep.tile([P, PACK, P, PACK], BF16, name="w_grouped", align_bytes=64)
+        w_dealt = keep.tile([P, PACK, PACK, P], BF16, name="w_dealt")
         nc.vector.tensor_copy(
-            w_grouped[:], w_raw[:].rearrange("p j (m t) -> p t m j", t=PACK)
+            w_dealt[:].rearrange("p j t m -> p j m t"), w_raw[:].rearrange("p j (m t) -> p j m t", t=PACK)
+        )
+        w_grouped = keep.tile([P, D, PACK], BF16, name="w_grouped", align_bytes=64)
+        nc.vector.tensor_copy(
+            w_grouped[:].rearrange("p (c i) j -> p c j i", i=4),
+            w_dealt[:].rearrange("p j t (c i) -> p (t c) j i", i=4),
         )
         w_codes = keep.tile([P, D], U32, name="w_codes", align_bytes=64)
         w_scales = keep.tile([P, D], U8, name="w_scales", align_bytes=64)
-        nc.vector.quantize_mx(w_codes[:].bitcast(E4M3), w_scales[:], w_grouped[:].rearrange("p t m j -> p (t m j)"))
+        nc.vector.quantize_mx(w_codes[:].bitcast(E4M3), w_scales[:], w_grouped[:].rearrange("p d j -> p (d j)"))
 
         ts_win = keep.tile([P, T], F32, name="ts_win", tag="ts_win")
         ts_lines = ts_win[:].rearrange("q (p b c) -> q b p c", p=P, c=BANK // P)
@@ -79,51 +87,54 @@ def tile_attend_gex_pl_x_kernel(tc, dyT, hT, ts, wm, offs, out_0, out_1, out_2):
 
         ts2 = keep.tile([P, N], F32, name="ts2")
         nc.scalar.activation(ts2[:], ts_win[:].indirect(offsets[:]), COPY, scale=2.0)
-        dz_first = keep.tile([P, PACK, HALF], F32, name="dz_first")
-        dz_second = keep.tile([P, PACK, HALF], BF16, name="dz_second")
+        dz = [keep.tile([P, PACK, HALF], BF16, name="dz%d" % half) for half in range(2)]
+        after_ts = keep.tile([P, 2, N], F32, name="after_ts", tag="ts_win")
 
-        h_picked = ring.tile([P, N], F32, name="h_picked")
-        nc.vector.tensor_copy(h_picked[:], h_win[0][:].indirect(offsets[:]))
-        dy_all = keep.tile([P, N], F32, name="dy_all")
-        nc.vector.tensor_copy(dy_all[:], dy_win[0][:].indirect(offsets[:]))
-        partial = ring.tile([P, N], F32, name="partial")
-        nc.vector.scalar_tensor_tensor(partial[:], h_picked[:], 0.0, dy_all[:], MAX, MULT)
-        nc.vector.tensor_tensor(dz_first[:, 0, :], partial[:, 0:HALF], ts2[:, 0:HALF], MULT)
-        nc.vector.tensor_tensor(dz_second[:, 0, :], partial[:, HALF:N], ts2[:, HALF:N], MULT)
+        def pick(picked, window, split):
+            nc.vector.tensor_copy(picked[:, 0:split], window[:].indirect(slots(0, split)))
+            if split < N:
+                nc.scalar.activation(picked[:, split:N], window[:].indirect(slots(split, N - split)), COPY)
 
-        for t in range(1, PACK):
-            if t == 1:
-                h_picked = keep.tile([P, N], F32, name="h_picked", tag="ts_win")
-            else:
-                h_picked = ring.tile([P, N], F32, name="h_picked")
-            if t < PACK - 1:
-                nc.scalar.activation(h_picked[:], h_win[t][:].indirect(offsets[:]), COPY)
-            else:
-                nc.vector.tensor_copy(h_picked[:, 0:HALF], h_win[t][:].indirect(slots(0, HALF)))
-                nc.scalar.activation(h_picked[:, HALF:N], h_win[t][:].indirect(slots(HALF, HALF)), COPY)
-            dy_picked = ring.tile([P, HALF], F32, name="dy_picked")
-            nc.scalar.activation(dy_picked[:], dy_win[t][:].indirect(slots(HALF, HALF)), COPY)
-            partial = ring.tile([P, N], F32, name="partial")
-            nc.vector.scalar_tensor_tensor(partial[:], h_picked[:], 0.0, ts2[:], MAX, MULT)
-            nc.vector.tensor_tensor(dz_first[:, t, :], dy_win[t][:].indirect(slots(0, HALF)), partial[:, 0:HALF], MULT)
-            if t < PACK - 1:
-                nc.vector.tensor_tensor(dz_second[:, t, :], dy_picked[:], partial[:, HALF:N], MULT)
+        def make_slope(t):
+            h_picked = after_ts[:, 1, :] if t == 1 else ring.tile([P, N], F32, name="h_picked")[:]
+            pick(h_picked, h_win[t], H_ON_VECTOR[t])
+            slope = ring.tile([P, N], F32, name="slope")
+            nc.vector.scalar_tensor_tensor(slope[:], h_picked, 0.0, ts2[:], MAX, MULT)
+            return slope
 
-        def group_dz(planes, half, copy):
+        def pick_dy(t):
+            dy_picked = after_ts[:, 0, :] if t == 0 else ring.tile([P, N], F32, name="dy_picked")[:]
+            pick(dy_picked, dy_win[t], DY_ON_VECTOR[t])
+            return dy_picked
+
+        def make_dz(t, half, slope, dy_picked):
+            cols = slice(half * HALF, (half + 1) * HALF)
+            nc.vector.tensor_tensor(dz[half][:, t, :], slope[:, cols], dy_picked[:, cols], MULT)
+
+        slope = make_slope(0)
+        for t in range(PACK - 1):
+            next_slope = make_slope(t + 1)
+            dy_picked = pick_dy(t)
+            for half in range(2):
+                make_dz(t, half, slope, dy_picked)
+            slope = next_slope
+        dy_picked = pick_dy(PACK - 1)
+
+        def group_dz(half, copy):
+            make_dz(PACK - 1, half, slope, dy_picked)
             grouped = keep.tile([P, HALF, PACK], BF16, name="grouped%d" % half, align_bytes=64)
-            copy(
-                grouped[:], planes[:].rearrange("p t s -> p s t")
-            )
+            copy(grouped[:].rearrange("p (c i) t -> p c t i", i=4), dz[half][:].rearrange("p t (c i) -> p c t i", i=4))
+            return grouped
+
+        def quantise_dz(grouped, half):
             codes = keep.tile([P, HALF], U32, name="dz_codes%d" % half, align_bytes=64)
             scales = keep.tile([P, HALF], U8, name="dz_scales%d" % half, align_bytes=64)
-            return grouped, codes, scales
+            nc.vector.quantize_mx(codes[:].bitcast(E5M2), scales[:], grouped[:].rearrange("p s t -> p (s t)"))
+            return codes, scales
 
-        nc.vector.tensor_tensor(dz_second[:, PACK - 1, :], dy_picked[:], partial[:, HALF:N], MULT)
-        first = group_dz(dz_first, 0, nc.vector.tensor_copy)
-        second = group_dz(dz_second, 1, nc.scalar.copy)
-        nc.vector.quantize_mx(first[1][:].bitcast(E5M2), first[2][:], first[0][:].rearrange("p s t -> p (s t)"))
-        nc.vector.quantize_mx(second[1][:].bitcast(E5M2), second[2][:], second[0][:].rearrange("p s t -> p (s t)"))
-        operands = (first, second)
+        second = group_dz(1, nc.scalar.copy)
+        first = group_dz(0, nc.vector.tensor_copy)
+        operands = (quantise_dz(first, 0), quantise_dz(second, 1))
 
         def product(t, half, tag):
             bank = single.tile([P, BANK], F32, name="product", tag=tag)
@@ -131,8 +142,8 @@ def tile_attend_gex_pl_x_kernel(tc, dyT, hT, ts, wm, offs, out_0, out_1, out_2):
                 bank[:],
                 lhsT=w_codes[:, t * P : (t + 1) * P].bitcast(E4M3),
                 lhsT_scale=w_scales[:, t * P : (t + 1) * P],
-                rhs=operands[half][1][:].bitcast(E5M2),
-                rhs_scale=operands[half][2][:],
+                rhs=operands[half][0][:].bitcast(E5M2),
+                rhs_scale=operands[half][1][:],
                 start=True,
                 stop=True,
             )
@@ -155,6 +166,20 @@ def tile_attend_gex_pl_x_kernel(tc, dyT, hT, ts, wm, offs, out_0, out_1, out_2):
             nc.vector.tensor_copy(dx[:], bank[:])
             nc.vector.tensor_copy(placed[t][:].indirect(slots(half * HALF, HALF)), dx[:])
 
+        shared_dx = keep.tile([P, SHARED + HALF], F32, name="shared_dx")
+
+        def shared_on_scalar(t):
+            bank = product(t, 0, "scalar_bank")
+            dx = ring.tile([P, HALF], F32, name="dx_scalar")
+            nc.scalar.copy(dx[:, 0 : HALF - SHARED], bank[:, 0 : HALF - SHARED])
+            nc.scalar.copy(shared_dx[:, 0:SHARED], bank[:, HALF - SHARED : HALF])
+            nc.scalar.activation(placed[t][:].indirect(slots(0, HALF - SHARED)), dx[:, 0 : HALF - SHARED], COPY)
+
+        def shared_on_vector(t):
+            bank = product(t, 1, "vector_bank")
+            nc.vector.tensor_copy(shared_dx[:, SHARED:], bank[:])
+            nc.vector.tensor_copy(placed[t][:].indirect(slots(HALF - SHARED, HALF + SHARED)), shared_dx[:])
+
         out_planes = out_0.rearrange("(p t) c -> t p c", t=PACK)
         pairs = [keep.tile([P, 2, CHUNK, 2], BF16, name="pairs%d" % c) for c in range(T // CHUNK)]
 
@@ -164,14 +189,14 @@ def tile_attend_gex_pl_x_kernel(tc, dyT, hT, ts, wm, offs, out_0, out_1, out_2):
                 nc.vector.tensor_copy(pairs[c][:, t // 2, :, t % 2], placed[t][:, c * CHUNK : (c + 1) * CHUNK])
 
         scatter_on_scalar(0, 0)
-        scatter_on_vector(1, 0)
-        scatter_on_scalar(0, 1)
         scatter_on_vector(1, 1)
-        scatter_on_scalar(2, 0)
+        scatter_on_scalar(0, 1)
+        scatter_on_vector(1, 0)
+        shared_on_scalar(2)
         hand_out(0)
         hand_out(1)
         scatter_on_scalar(3, 0)
-        scatter_on_vector(2, 1)
+        shared_on_vector(2)
         scatter_on_scalar(3, 1)
         hand_out(2)
         hand_out(3)
@@ -180,9 +205,10 @@ def tile_attend_gex_pl_x_kernel(tc, dyT, hT, ts, wm, offs, out_0, out_1, out_2):
         y_scales = keep.tile([P, T], U8, name="y_scales", align_bytes=64)
         for c in range(T // CHUNK):
             y_grouped = keep.tile([P, CHUNK * PACK], BF16, name="y_grouped%d" % c, align_bytes=64)
-            nc.scalar.copy(
-                y_grouped[:].bitcast(U32).rearrange("p (s u) -> p s u", u=2),
-                pairs[c][:].rearrange("p u s e -> p u (s e)").bitcast(U32).rearrange("p u s -> p s u"),
+            copy, word = (nc.vector.tensor_copy, I32) if c == T // CHUNK - 1 else (nc.scalar.copy, U32)
+            copy(
+                y_grouped[:].bitcast(word).rearrange("p (s u) -> p s u", u=2),
+                pairs[c][:].rearrange("p u s e -> p u (s e)").bitcast(word).rearrange("p u s -> p s u"),
             )
             y_codes = keep.tile([P, CHUNK], U32, name="y_codes%d" % c, align_bytes=64)
             nc.vector.quantize_mx(y_codes[:].bitcast(E4M3), y_scales[:, c * CHUNK : (c + 1) * CHUNK], y_grouped[:])

@@ -26,7 +26,7 @@ PIECE = 256
 CHUNK = 512
 H_ON_VECTOR = (N, 256, 256, 384)
 DY_ON_VECTOR = (384, 384, 384, HALF)
-SHARED = 256
+SHARED = 192
 
 
 def tile_attend_gex_pl_x_kernel(tc, dyT, hT, ts, wm, offs, out_0, out_1, out_2):
@@ -61,7 +61,11 @@ def tile_attend_gex_pl_x_kernel(tc, dyT, hT, ts, wm, offs, out_0, out_1, out_2):
         placed = []
         for t in range(PACK):
             placed.append(keep.tile([P, T], F32, name="placed%d" % t))
-            nc.vector.memset(placed[t][:].bitcast(I32), 0)
+            if t < 2:
+                nc.vector.memset(placed[t][:], 0.0)
+            else:
+                nc.gpsimd.memset(placed[t][:, 0 : T // 2], 0.0)
+                nc.gpsimd.memset(placed[t][:, T // 2 : T], 0.0)
 
         w_dealt = keep.tile([P, PACK, PACK, P], BF16, name="w_dealt")
         nc.vector.tensor_copy(
@@ -88,7 +92,7 @@ def tile_attend_gex_pl_x_kernel(tc, dyT, hT, ts, wm, offs, out_0, out_1, out_2):
         ts2 = keep.tile([P, N], F32, name="ts2")
         nc.scalar.activation(ts2[:], ts_win[:].indirect(offsets[:]), COPY, scale=2.0)
         dz = [keep.tile([P, PACK, HALF], BF16, name="dz%d" % half) for half in range(2)]
-        after_ts = keep.tile([P, 2, N], F32, name="after_ts", tag="ts_win")
+        after_ts = keep.tile([P, 4, N], F32, name="after_ts", tag="ts_win")
 
         def pick(picked, window, split):
             nc.vector.tensor_copy(picked[:, 0:split], window[:].indirect(slots(0, split)))
@@ -96,14 +100,14 @@ def tile_attend_gex_pl_x_kernel(tc, dyT, hT, ts, wm, offs, out_0, out_1, out_2):
                 nc.scalar.activation(picked[:, split:N], window[:].indirect(slots(split, N - split)), COPY)
 
         def make_slope(t):
-            h_picked = after_ts[:, 1, :] if t == 1 else ring.tile([P, N], F32, name="h_picked")[:]
+            h_picked = after_ts[:, t - 1, :] if t in (1, 2) else ring.tile([P, N], F32, name="h_picked")[:]
             pick(h_picked, h_win[t], H_ON_VECTOR[t])
             slope = ring.tile([P, N], F32, name="slope")
             nc.vector.scalar_tensor_tensor(slope[:], h_picked, 0.0, ts2[:], MAX, MULT)
             return slope
 
         def pick_dy(t):
-            dy_picked = after_ts[:, 0, :] if t == 0 else ring.tile([P, N], F32, name="dy_picked")[:]
+            dy_picked = after_ts[:, 2 + t, :] if t < 2 else ring.tile([P, N], F32, name="dy_picked")[:]
             pick(dy_picked, dy_win[t], DY_ON_VECTOR[t])
             return dy_picked
 

from contextlib import ExitStack

import concourse.mybir as mybir
from concourse.masks import make_identity

T, N, D, DV = 2048, 1024, 512, 512
FLOPS = 2 * N * D * DV

F32 = mybir.dt.float32
BF16 = mybir.dt.bfloat16
I32 = mybir.dt.int32
U32 = mybir.dt.uint32
U16 = mybir.dt.uint16
U8 = mybir.dt.uint8
E4M3 = mybir.dt.float8_e4m3fn_x4
E5M2 = mybir.dt.float8_e5m2_x4
COPY = mybir.ActivationFunctionType.Copy
MULT = mybir.AluOpType.mult
MAX = mybir.AluOpType.max

P = 128
PACK = 4
HALF = N // 2
BANK = 512
PIECE = 256
CHUNK = 512
H_ON_VECTOR = (N, 256, 256, 384)
DY_ON_VECTOR = (384, 384, 384, HALF)
SHARED = 192


def tile_attend_gex_pl_x_kernel(tc, dyT, hT, ts, wm, offs, out_0, out_1, out_2):
    nc = tc.nc
    with ExitStack() as ctx:
        keep = ctx.enter_context(tc.tile_pool(name="keep", bufs=1))
        ring = ctx.enter_context(tc.tile_pool(name="ring", bufs=2))
        psum = ctx.enter_context(tc.psum_pool(name="psum", bufs=4))
        single = ctx.enter_context(tc.psum_pool(name="single", bufs=1))

        def slots(first, count):
            return offsets[:, first // 16 : (first + count) // 16]

        offsets = keep.tile([P, N // 16], U16, name="offsets")
        nc.sync.dma_start(offsets[:], offs)
        ts_cols = keep.tile([P, T // P], F32, name="ts_cols")
        nc.sync.dma_start(ts_cols[:], ts[0].rearrange("(p c) -> p c", p=P))
        w_raw = keep.tile([P, PACK, D], F32, name="w_raw")
        nc.sync.dma_start(w_raw[:], wm[0].rearrange("(p j) d -> p j d", j=PACK))
        h_planes = hT.rearrange("(p t) c -> t p c", t=PACK)
        dy_planes = dyT.rearrange("(p t) c -> t p c", t=PACK)
        h_win = [keep.tile([P, T], F32, name="h_win%d" % t) for t in range(PACK)]
        dy_win = [keep.tile([P, T], F32, name="dy_win%d" % t) for t in range(PACK)]
        for step in range(PACK + 1):
            if step < PACK:
                nc.sync.dma_start(h_win[step][:], h_planes[step])
            if step > 0:
                nc.sync.dma_start(dy_win[step - 1][:], dy_planes[step - 1])

        identity = keep.tile([P, P], F32, name="identity")
        make_identity(nc, identity[:])
        placed = []
        for t in range(PACK):
            placed.append(keep.tile([P, T], F32, name="placed%d" % t))
            if t < 2:
                nc.vector.memset(placed[t][:], 0.0)
            else:
                nc.gpsimd.memset(placed[t][:, 0 : T // 2], 0.0)
                nc.gpsimd.memset(placed[t][:, T // 2 : T], 0.0)

        w_dealt = keep.tile([P, PACK, PACK, P], BF16, name="w_dealt")
        nc.vector.tensor_copy(
            w_dealt[:].rearrange("p j t m -> p j m t"), w_raw[:].rearrange("p j (m t) -> p j m t", t=PACK)
        )
        w_grouped = keep.tile([P, D, PACK], BF16, name="w_grouped", align_bytes=64)
        nc.vector.tensor_copy(
            w_grouped[:].rearrange("p (c i) j -> p c j i", i=4),
            w_dealt[:].rearrange("p j t (c i) -> p (t c) j i", i=4),
        )
        w_codes = keep.tile([P, D], U32, name="w_codes", align_bytes=64)
        w_scales = keep.tile([P, D], U8, name="w_scales", align_bytes=64)
        nc.vector.quantize_mx(w_codes[:].bitcast(E4M3), w_scales[:], w_grouped[:].rearrange("p d j -> p (d j)"))

        ts_win = keep.tile([P, T], F32, name="ts_win", tag="ts_win")
        ts_lines = ts_win[:].rearrange("q (p b c) -> q b p c", p=P, c=BANK // P)
        for b in range(T // BANK):
            spread = psum.tile([P, BANK // P, P], F32, name="spread")
            for c in range(BANK // P):
                col = b * (BANK // P) + c
                nc.tensor.transpose(spread[:, c, :], ts_cols[:, col : col + 1].to_broadcast([P, P]), identity[:])
            nc.scalar.activation(ts_lines[:, b], spread[:].rearrange("q c p -> q p c"), COPY)

        ts2 = keep.tile([P, N], F32, name="ts2")
        nc.scalar.activation(ts2[:], ts_win[:].indirect(offsets[:]), COPY, scale=2.0)
        dz = [keep.tile([P, PACK, HALF], BF16, name="dz%d" % half) for half in range(2)]
        after_ts = keep.tile([P, 4, N], F32, name="after_ts", tag="ts_win")

        def pick(picked, window, split):
            nc.vector.tensor_copy(picked[:, 0:split], window[:].indirect(slots(0, split)))
            if split < N:
                nc.scalar.activation(picked[:, split:N], window[:].indirect(slots(split, N - split)), COPY)

        def make_slope(t):
            h_picked = after_ts[:, t - 1, :] if t in (1, 2) else ring.tile([P, N], F32, name="h_picked")[:]
            pick(h_picked, h_win[t], H_ON_VECTOR[t])
            slope = ring.tile([P, N], F32, name="slope")
            nc.vector.scalar_tensor_tensor(slope[:], h_picked, 0.0, ts2[:], MAX, MULT)
            return slope

        def pick_dy(t):
            dy_picked = after_ts[:, 2 + t, :] if t < 2 else ring.tile([P, N], F32, name="dy_picked")[:]
            pick(dy_picked, dy_win[t], DY_ON_VECTOR[t])
            return dy_picked

        def make_dz(t, half, slope, dy_picked):
            cols = slice(half * HALF, (half + 1) * HALF)
            nc.vector.tensor_tensor(dz[half][:, t, :], slope[:, cols], dy_picked[:, cols], MULT)

        slope = make_slope(0)
        for t in range(PACK - 1):
            next_slope = make_slope(t + 1)
            dy_picked = pick_dy(t)
            for half in range(2):
                make_dz(t, half, slope, dy_picked)
            slope = next_slope
        dy_picked = pick_dy(PACK - 1)

        def group_dz(half, copy):
            make_dz(PACK - 1, half, slope, dy_picked)
            grouped = keep.tile([P, HALF, PACK], BF16, name="grouped%d" % half, align_bytes=64)
            copy(grouped[:].rearrange("p (c i) t -> p c t i", i=4), dz[half][:].rearrange("p t (c i) -> p c t i", i=4))
            return grouped

        def quantise_dz(grouped, half):
            codes = keep.tile([P, HALF], U32, name="dz_codes%d" % half, align_bytes=64)
            scales = keep.tile([P, HALF], U8, name="dz_scales%d" % half, align_bytes=64)
            nc.vector.quantize_mx(codes[:].bitcast(E5M2), scales[:], grouped[:].rearrange("p s t -> p (s t)"))
            return codes, scales

        second = group_dz(1, nc.scalar.copy)
        first = group_dz(0, nc.vector.tensor_copy)
        operands = (quantise_dz(first, 0), quantise_dz(second, 1))

        def product(t, half, tag):
            bank = single.tile([P, BANK], F32, name="product", tag=tag)
            nc.tensor.matmul_mx(
                bank[:],
                lhsT=w_codes[:, t * P : (t + 1) * P].bitcast(E4M3),
                lhsT_scale=w_scales[:, t * P : (t + 1) * P],
                rhs=operands[half][0][:].bitcast(E5M2),
                rhs_scale=operands[half][1][:],
                start=True,
                stop=True,
            )
            return bank

        def scatter_on_scalar(t, half):
            bank = product(t, half, "scalar_bank")
            dx = ring.tile([P, HALF], F32, name="dx_scalar")
            nc.scalar.copy(dx[:], bank[:])
            for first_slot in range(0, HALF, PIECE):
                nc.scalar.activation(
                    placed[t][:].indirect(slots(half * HALF + first_slot, PIECE)),
                    dx[:, first_slot : first_slot + PIECE],
                    COPY,
                )

        def scatter_on_vector(t, half):
            bank = product(t, half, "vector_bank")
            dx = ring.tile([P, HALF], F32, name="dx_vector")
            nc.vector.tensor_copy(dx[:], bank[:])
            nc.vector.tensor_copy(placed[t][:].indirect(slots(half * HALF, HALF)), dx[:])

        shared_dx = keep.tile([P, SHARED + HALF], F32, name="shared_dx")

        def shared_on_scalar(t):
            bank = product(t, 0, "scalar_bank")
            dx = ring.tile([P, HALF], F32, name="dx_scalar")
            nc.scalar.copy(dx[:, 0 : HALF - SHARED], bank[:, 0 : HALF - SHARED])
            nc.scalar.copy(shared_dx[:, 0:SHARED], bank[:, HALF - SHARED : HALF])
            nc.scalar.activation(placed[t][:].indirect(slots(0, HALF - SHARED)), dx[:, 0 : HALF - SHARED], COPY)

        def shared_on_vector(t):
            bank = product(t, 1, "vector_bank")
            nc.vector.tensor_copy(shared_dx[:, SHARED:], bank[:])
            nc.vector.tensor_copy(placed[t][:].indirect(slots(HALF - SHARED, HALF + SHARED)), shared_dx[:])

        out_planes = out_0.rearrange("(p t) c -> t p c", t=PACK)
        pairs = [keep.tile([P, 2, CHUNK, 2], BF16, name="pairs%d" % c) for c in range(T // CHUNK)]

        def hand_out(t):
            nc.sync.dma_start(out_planes[t], placed[t][:])
            for c in range(T // CHUNK):
                nc.vector.tensor_copy(pairs[c][:, t // 2, :, t % 2], placed[t][:, c * CHUNK : (c + 1) * CHUNK])

        scatter_on_scalar(0, 0)
        scatter_on_vector(1, 1)
        scatter_on_scalar(0, 1)
        scatter_on_vector(1, 0)
        shared_on_scalar(2)
        hand_out(0)
        hand_out(1)
        scatter_on_scalar(3, 0)
        shared_on_vector(2)
        scatter_on_scalar(3, 1)
        hand_out(2)
        hand_out(3)

        out_words = out_1[0].rearrange("p t l -> p (t l)").bitcast(I32)
        y_scales = keep.tile([P, T], U8, name="y_scales", align_bytes=64)
        for c in range(T // CHUNK):
            y_grouped = keep.tile([P, CHUNK * PACK], BF16, name="y_grouped%d" % c, align_bytes=64)
            copy, word = (nc.vector.tensor_copy, I32) if c == T // CHUNK - 1 else (nc.scalar.copy, U32)
            copy(
                y_grouped[:].bitcast(word).rearrange("p (s u) -> p s u", u=2),
                pairs[c][:].rearrange("p u s e -> p u (s e)").bitcast(word).rearrange("p u s -> p s u"),
            )
            y_codes = keep.tile([P, CHUNK], U32, name="y_codes%d" % c, align_bytes=64)
            nc.vector.quantize_mx(y_codes[:].bitcast(E4M3), y_scales[:, c * CHUNK : (c + 1) * CHUNK], y_grouped[:])
            nc.sync.dma_start(out_words[:, c * CHUNK : (c + 1) * CHUNK], y_codes[:].bitcast(I32))
        scale_rows = out_2[0].bitcast(I32)
        for q in range(4):
            nc.sync.dma_start(scale_rows[4 * q : 4 * q + 4, :], y_scales[32 * q : 32 * q + 4, :].bitcast(I32))
